import numpy as np, ml_dtypes
CORES = [4,12,20,28,44,60,76,84,92,108,116,124]
N = 12
S, B = 2, 512
def setup_inputs(rng):
    a = (rng.standard_normal((128, 128), dtype=np.float32) / 12).astype(ml_dtypes.bfloat16)
    return {"x": rng.standard_normal((N, 128, S * B), dtype=np.float32).astype(ml_dtypes.bfloat16), "a": np.broadcast_to(a, (N, 128, 128)).copy(), "at": np.broadcast_to(a.T, (N, 128, 128)).copy()}
def setup_inputs_big(rng):
    d = setup_inputs(rng)
    for k in ("x",): d[k] = (d[k].astype(np.float32) * 1048576.0).astype(d[k].dtype)
    return d
def setup_inputs_small(rng):
    d = setup_inputs(rng)
    for k in ("x",): d[k] = (d[k].astype(np.float32) * (1 / 1048576.0)).astype(d[k].dtype)
    return d
def setup_inputs_apart(rng):
    d = setup_inputs(rng)
    f = (10.0 ** rng.permutation(np.linspace(-1.5, 1.5, N))).astype(np.float32).reshape(N, 1, 1)
    for k in ("x",): d[k] = (d[k].astype(np.float32) * f).astype(d[k].dtype)
    return d
def reference(x, a, at):
    X, A = x.astype(np.float64), a.astype(np.float64)
    y = np.zeros((N, 128, S * B)); h = np.zeros((128, B))
    for r in range(N):
        for s in range(S):
            h = A[r].T @ h + X[r][:, B * s:B * s + B]
            y[r][:, B * s:B * s + B] = h
    return {"y": y.astype(ml_dtypes.bfloat16)}

@@ -1,0 +1,229 @@
+from concourse.bass import DstId, RemoteDMATransfer
+from concourse.mybir import AluOpType
+
+LANES = 4
+WIN = 4
+B = 512
+W = B // LANES
+F = 128
+NPOOL = 40
+
+Q1, P1, P2, P9, P10, P17, P18, Q2, P4, Q4, Q8 = range(11)
+P6 = Q4
+
+SCRATCH = {
+    "mats": ("sbuf", [F, 11 * F], "bfloat16"),
+    "xs": ("sbuf", [F, 2 * B], "bfloat16"),
+    "cs": ("sbuf", [F, B], "bfloat16"),
+    "sland": ("sbuf", [F, 3 * B], "bfloat16"),
+    "ys": ("sbuf", [F, 2 * B], "bfloat16"),
+    "cq": ("sbuf", [F, WIN * W], "bfloat16"),
+    "sq": ("sbuf", [F, W], "bfloat16"),
+}
+for _b in range(8):
+    SCRATCH["ps%d" % _b] = ("psum", [F, 512], "float32")
+
+SEMAPHORES = (["ld_a", "ld_x0", "ld_x1", "c_done", "y0_done", "y1_done", "st", "sent", "a_arr", "c_arr", "r1", "sq_done"]
+              + ["s%d_%d" % (k, q) for k in range(3) for q in range(LANES)]
+              + ["k%d" % i for i in range(NPOOL)])
+
+
+def rank_program(g, core, T, topo):
+    cores = list(T.cores)
+    n = len(cores)
+    every = range(topo.CORES_PER_CHIP * topo.CHIPS)
+
+    def lanes_of(j):
+        home = cores[j]
+        cand = [c for c in every
+                if topo.chip(c) == topo.chip(home) and c != home
+                and all(topo.may_write(c, d) for d in cores if d != c)]
+        cand.sort(key=lambda c: (topo.die(c) != topo.die(home), c))
+        return cand[:LANES]
+
+    def engines(dsts, first, count):
+        m = topo.mask(core, dsts[0])
+        for d in dsts[1:]:
+            m &= topo.mask(core, d)
+        bits = [1 << i for i in range(m.bit_length()) if (m >> i) & 1]
+        return sum(bits[first:first + count])
+
+    def dst_of(c):
+        rid, pid, _se = topo.addr(c)
+        return DstId(rid=rid, pnc=pid)
+
+    def blk(t, k, w=W, cnt=1):
+        return t[:, k * w:(k + cnt) * w]
+
+    pool = [0]
+    seen = {"pe": set(), "ve": set()}
+    ready = {}
+    bank_free = {}
+
+    def fresh():
+        pool[0] += 1
+        return "k%d" % (pool[0] - 1)
+
+    def wait(q, dep):
+        if dep not in seen[q]:
+            seen[q].add(dep)
+            (g.tensor if q == "pe" else g.vector).wait_ge(T.sem[dep[0]], dep[1])
+
+    def ps(b, cols=W):
+        return T["ps%d" % b][:, 0:cols]
+
+    def power(bank, lhs, rhs, cnt, out):
+        for s in [lhs] + list(range(rhs, rhs + cnt)):
+            wait("pe", ready[s])
+        if bank in bank_free:
+            wait("pe", bank_free[bank])
+        m, d = fresh(), fresh()
+        g.tensor.matmul(ps(bank, cnt * F), blk(T.mats, lhs, F), blk(T.mats, rhs, F, cnt), True, True).then_inc(T.sem[m], 1)
+        wait("ve", (m, 1))
+        g.vector.tensor_copy(blk(T.mats, out, F, cnt), ps(bank, cnt * F)).then_inc(T.sem[d], 1)
+        for s in range(out, out + cnt):
+            ready[s] = (d, 1)
+        bank_free[bank] = (d, 1)
+
+    rank = T.rank_of(core)
+
+    if rank is None:
+        where = [(j, q) for j in range(n - 1) for q, c in enumerate(lanes_of(j)) if c == core]
+        if not where:
+            return
+        j, q = where[0]
+        nsrc = min(WIN - 1, j)
+        nxt = [d for d in range(1, WIN) if j + d <= n - 2]
+        use = [m for m in range(3) if j + 1 + WIN * m <= n - 1]
+        sent = 0
+
+        g.wait_ge(T.sem.c_arr, 16 // LANES)
+        if nxt:
+            to = [lanes_of(j + d)[q] for d in nxt]
+            g.remote_dma_fused([RemoteDMATransfer(
+                dst_ids=[dst_of(c) for c in to], dma_engine_mask=engines(to, 0, 8), remote_sem=T.sem.r1,
+                srcs=[blk(T.cq, 0)], dsts=[blk(T.cq, d) for d in nxt], alu_op=0)], local_sem=T.sem.sent)
+            sent += 8
+
+        if nsrc:
+            ready[Q1] = ready[P1] = ("a_arr", 16 // LANES)
+            power(4, Q1, P1, 1, P2)
+            if nsrc >= 2:
+                power(5, P1, Q1, 1, Q2)
+                power(6, Q2, P2, 1, P4)
+            if nsrc >= 3:
+                power(7, Q2, P4, 1, P6)
+            wait("pe", ("r1", 8 * nsrc))
+            m = fresh()
+            for d in range(1, nsrc + 1):
+                lhs = (P2, P4, P6)[d - 1]
+                wait("pe", ready[lhs])
+                mm = g.tensor.matmul(ps(0), blk(T.mats, lhs, F), blk(T.cq, d), d == 1, d == nsrc)
+            mm.then_inc(T.sem[m], 1)
+            wait("ve", ("c_arr", 16 // LANES))
+            wait("ve", (m, 1))
+            g.vector.tensor_tensor(T.sq[:, :], ps(0), blk(T.cq, 0), AluOpType.add).then_inc(T.sem.sq_done, 1)
+            g.wait_ge(T.sem.sq_done, 1)
+            src = T.sq[:, :]
+        else:
+            src = blk(T.cq, 0)
+
+        to = [cores[j + 1 + WIN * m] for m in use]
+        g.remote_dma_fused([RemoteDMATransfer(
+            dst_ids=[dst_of(c) for c in to], dma_engine_mask=engines(to, 0, 8),
+            remote_sem=T.sem["s%d_%d" % (j // WIN, q)],
+            srcs=[src], dsts=[blk(T.sland, m * LANES + q) for m in use], alu_op=0)], local_sem=T.sem.sent)
+        sent += 8
+        g.wait_ge(T.sem.sent, sent)
+        return
+
+    r = rank
+    need_at = r >= 1
+    g.sync.dma_start(blk(T.mats, P1, F), T.a[:, :]).then_inc(T.sem.ld_a, 16)
+    if need_at:
+        g.scalar.dma_start(blk(T.mats, Q1, F), T.at[:, :]).then_inc(T.sem.ld_a, 16)
+    g.sync.dma_start(T.xs[:, 0:B], T.x[:, 0:B]).then_inc(T.sem.ld_x0, 16)
+    g.scalar.dma_start(T.xs[:, B:2 * B], T.x[:, B:2 * B]).then_inc(T.sem.ld_x1, 16)
+    got_a = ("ld_a", 32 if need_at else 16)
+    ready[Q1] = ready[P1] = got_a
+
+    sent = 0
+    per = 16 // LANES
+    mine = lanes_of(r) if r <= n - 2 else []
+    if mine and r >= 1:
+        g.wait_ge(T.sem[got_a[0]], got_a[1])
+        g.remote_dma_fused([RemoteDMATransfer(
+            dst_ids=[dst_of(c)], dma_engine_mask=engines([c], per * q, per), remote_sem=T.sem.a_arr,
+            srcs=[blk(T.mats, Q1, F, 2)], dsts=[blk(T.mats, Q1, F, 2)], alu_op=0)
+            for q, c in enumerate(mine)], local_sem=T.sem.sent)
+        sent += 16
+
+    wait("pe", got_a)
+    wait("pe", ("ld_x0", 16))
+    wait("ve", ("ld_x1", 16))
+    for q in range(LANES):
+        m = fresh()
+        g.tensor.matmul(ps(q), blk(T.mats, P1, F), blk(T.xs, q), True, True).then_inc(T.sem[m], 1)
+        wait("ve", (m, 1))
+        g.vector.tensor_tensor(blk(T.cs, q), ps(q), blk(T.xs, LANES + q), AluOpType.add).then_inc(T.sem.c_done, 1)
+        bank_free[q] = ("c_done", LANES)
+
+    if mine:
+        g.wait_ge(T.sem.c_done, LANES)
+        g.remote_dma_fused([RemoteDMATransfer(
+            dst_ids=[dst_of(c)], dma_engine_mask=engines([c], per * q, per), remote_sem=T.sem.c_arr,
+            srcs=[blk(T.cs, q)], dsts=[blk(T.cq, 0)], alu_op=0)
+            for q, c in enumerate(mine)], local_sem=T.sem.sent)
+        sent += 16
+
+    if r == 0:
+        g.sync.wait_ge(T.sem.ld_x0, 16)
+        g.sync.dma_start(T.y[:, 0:B], T.xs[:, 0:B]).then_inc(T.sem.st, 16)
+        g.scalar.wait_ge(T.sem.c_done, LANES)
+        g.scalar.dma_start(T.y[:, B:2 * B], T.cs[:, :]).then_inc(T.sem.st, 16)
+        g.wait_ge(T.sem.sent, sent)
+        g.wait_ge(T.sem.st, 32)
+        return
+
+    nm = len([m for m in range(3) if r - 1 - WIN * m >= 0])
+    power(4, Q1, P1, 1, P2)
+    if nm >= 2:
+        power(5, P1, Q1, 1, Q2)
+        power(6, Q2, P2, 1, P4)
+        power(7, P2, Q2, 1, Q4)
+        power(4, P4, Q4, 1, Q8)
+        power(5, Q8, P1, 2, P9)
+    if nm >= 3:
+        power(6, Q8, P9, 2, P17)
+
+    fin = {}
+    for m in reversed(range(nm)):
+        jsrc = r - 1 - WIN * m
+        for inst in range(2):
+            for q in range(LANES):
+                bank = inst * LANES + q
+                lhs = P1 + 2 * m + inst
+                wait("pe", ready[lhs])
+                if bank in bank_free:
+                    wait("pe", bank_free[bank])
+                wait("pe", ("s%d_%d" % (jsrc // WIN, q), 8))
+                mm = g.tensor.matmul(ps(bank), blk(T.mats, lhs, F), blk(T.sland, m * LANES + q), m == nm - 1, m == 0)
+                if m == 0:
+                    fin[bank] = fresh()
+                    mm.then_inc(T.sem[fin[bank]], 1)
+    wait("ve", ("ld_x0", 16))
+    wait("ve", ("c_done", LANES))
+    for inst in range(2):
+        for q in range(LANES):
+            bank = inst * LANES + q
+            wait("ve", (fin[bank], 1))
+            local = blk(T.xs, q) if inst == 0 else blk(T.cs, q)
+            g.vector.tensor_tensor(blk(T.ys, bank), ps(bank), local, AluOpType.add).then_inc(
+                T.sem.y0_done if inst == 0 else T.sem.y1_done, 1)
+    g.sync.wait_ge(T.sem.y0_done, LANES)
+    g.sync.dma_start(T.y[:, 0:B], T.ys[:, 0:B]).then_inc(T.sem.st, 16)
+    g.scalar.wait_ge(T.sem.y1_done, LANES)
+    g.scalar.dma_start(T.y[:, B:2 * B], T.ys[:, B:2 * B]).then_inc(T.sem.st, 16)
+    if sent:
+        g.wait_ge(T.sem.sent, sent)
+    g.wait_ge(T.sem.st, 32)

@@ -6,13 +6,16 @@ WIN = 4
 B = 512
 W = B // LANES
 F = 128
-NPOOL = 40
+NPOOL = 48
+ENGS = 8
+ENG1 = 8
+ENG2 = 8
 
-Q1, P1, P2, P9, P10, P17, P18, Q2, P4, Q4, Q8 = range(11)
+Q1, P1, P2, P9, P17, Q2, P4, Q4, Q8 = range(9)
 P6 = Q4
 
 SCRATCH = {
-    "mats": ("sbuf", [F, 11 * F], "bfloat16"),
+    "mats": ("sbuf", [F, 9 * F], "bfloat16"),
     "xs": ("sbuf", [F, 2 * B], "bfloat16"),
     "cs": ("sbuf", [F, B], "bfloat16"),
     "sland": ("sbuf", [F, 3 * B], "bfloat16"),
@@ -23,7 +26,8 @@ SCRATCH = {
 for _b in range(8):
     SCRATCH["ps%d" % _b] = ("psum", [F, 512], "float32")
 
-SEMAPHORES = (["ld_a", "ld_x0", "ld_x1", "c_done", "y0_done", "y1_done", "st", "sent", "a_arr", "c_arr", "r1", "sq_done"]
+SEMAPHORES = (["ld_a", "ld_at", "ld_x0", "ld_x1", "c_done", "st", "sent", "a0", "a1", "c_arr", "sq_done"]
+              + ["r1_%d" % k for k in range(WIN - 1)]
               + ["s%d_%d" % (k, q) for k in range(3) for q in range(LANES)]
               + ["k%d" % i for i in range(NPOOL)])
 
@@ -32,6 +36,7 @@ def rank_program(g, core, T, topo):
     cores = list(T.cores)
     n = len(cores)
     every = range(topo.CORES_PER_CHIP * topo.CHIPS)
+    per = 16 // LANES
 
     def lanes_of(j):
         home = cores[j]
@@ -41,12 +46,24 @@ def rank_program(g, core, T, topo):
         cand.sort(key=lambda c: (topo.die(c) != topo.die(home), c))
         return cand[:LANES]
 
-    def engines(dsts, first, count):
+    def a_part(j, q):
+        pos = q % 2
+        if j == 0:
+            lo, wd = F // 2, F // 2
+        elif j == 1:
+            lo, wd = pos * (F // 4), F // 4
+        else:
+            lo, wd = pos * (F // 2), F // 2
+        return T.mats[:, P1 * F + lo:P1 * F + lo + wd]
+
+    def bits_of(dsts):
         m = topo.mask(core, dsts[0])
         for d in dsts[1:]:
             m &= topo.mask(core, d)
-        bits = [1 << i for i in range(m.bit_length()) if (m >> i) & 1]
-        return sum(bits[first:first + count])
+        return [1 << i for i in range(m.bit_length()) if (m >> i) & 1]
+
+    def engines(dsts, count):
+        return sum(bits_of(dsts)[:count])
 
     def dst_of(c):
         rid, pid, _se = topo.addr(c)
@@ -56,7 +73,8 @@ def rank_program(g, core, T, topo):
         return t[:, k * w:(k + cnt) * w]
 
     pool = [0]
-    seen = {"pe": set(), "ve": set()}
+    queues = {"pe": g.tensor, "ve": g.vector, "g": g, "sy": g.sync, "sc": g.scalar}
+    seen = set()
     ready = {}
     bank_free = {}
 
@@ -65,24 +83,23 @@ def rank_program(g, core, T, topo):
         return "k%d" % (pool[0] - 1)
 
     def wait(q, dep):
-        if dep not in seen[q]:
-            seen[q].add(dep)
-            (g.tensor if q == "pe" else g.vector).wait_ge(T.sem[dep[0]], dep[1])
+        if (q, dep) not in seen:
+            seen.add((q, dep))
+            queues[q].wait_ge(T.sem[dep[0]], dep[1])
 
     def ps(b, cols=W):
         return T["ps%d" % b][:, 0:cols]
 
-    def power(bank, lhs, rhs, cnt, out):
-        for s in [lhs] + list(range(rhs, rhs + cnt)):
-            wait("pe", ready[s])
+    def power(bank, lhs, rhs, out):
+        wait("pe", ready[lhs])
+        wait("pe", ready[rhs])
         if bank in bank_free:
             wait("pe", bank_free[bank])
         m, d = fresh(), fresh()
-        g.tensor.matmul(ps(bank, cnt * F), blk(T.mats, lhs, F), blk(T.mats, rhs, F, cnt), True, True).then_inc(T.sem[m], 1)
+        g.tensor.matmul(ps(bank, F), blk(T.mats, lhs, F), blk(T.mats, rhs, F), True, True).then_inc(T.sem[m], 1)
         wait("ve", (m, 1))
-        g.vector.tensor_copy(blk(T.mats, out, F, cnt), ps(bank, cnt * F)).then_inc(T.sem[d], 1)
-        for s in range(out, out + cnt):
-            ready[s] = (d, 1)
+        g.vector.tensor_copy(blk(T.mats, out, F), ps(bank, F)).then_inc(T.sem[d], 1)
+        ready[out] = (d, 1)
         bank_free[bank] = (d, 1)
 
     rank = T.rank_of(core)
@@ -94,136 +111,156 @@ def rank_program(g, core, T, topo):
         j, q = where[0]
         nsrc = min(WIN - 1, j)
         nxt = [d for d in range(1, WIN) if j + d <= n - 2]
-        use = [m for m in range(3) if j + 1 + WIN * m <= n - 1]
+        use = [m for m in reversed(range(3)) if j + 1 + WIN * m <= n - 1]
         sent = 0
 
-        g.wait_ge(T.sem.c_arr, 16 // LANES)
+        onto = lanes_of(1)[q] if j == 0 else lanes_of(j)[q + 1 - 2 * (q % 2)]
+        wait("g", ("a0", per))
+        g.remote_dma_fused([RemoteDMATransfer(
+            dst_ids=[dst_of(onto)], dma_engine_mask=engines([onto, cores[j + 1]], ENGS), remote_sem=T.sem.a1,
+            srcs=[a_part(j, q)], dsts=[a_part(j, q)], alu_op=0)], local_sem=T.sem.sent)
+        sent += ENGS
+
+        wait("g", ("c_arr", per))
         if nxt:
             to = [lanes_of(j + d)[q] for d in nxt]
             g.remote_dma_fused([RemoteDMATransfer(
-                dst_ids=[dst_of(c) for c in to], dma_engine_mask=engines(to, 0, 8), remote_sem=T.sem.r1,
+                dst_ids=[dst_of(c) for c in to], dma_engine_mask=engines(to, ENG1),
+                remote_sem=T.sem["r1_%d" % (j % (WIN - 1))],
                 srcs=[blk(T.cq, 0)], dsts=[blk(T.cq, d) for d in nxt], alu_op=0)], local_sem=T.sem.sent)
-            sent += 8
+            sent += ENG1
 
         if nsrc:
-            ready[Q1] = ready[P1] = ("a_arr", 16 // LANES)
-            power(4, Q1, P1, 1, P2)
+            wait("pe", ("a0", per))
+            ready[Q1] = ready[P1] = ("a1", ENGS * (2 if j == 1 else 1) + per)
+            power(4, Q1, P1, P2)
             if nsrc >= 2:
-                power(5, P1, Q1, 1, Q2)
-                power(6, Q2, P2, 1, P4)
+                power(5, P1, Q1, Q2)
+                power(6, Q2, P2, P4)
             if nsrc >= 3:
-                power(7, Q2, P4, 1, P6)
-            wait("pe", ("r1", 8 * nsrc))
+                power(7, Q2, P4, P6)
             m = fresh()
             for d in range(1, nsrc + 1):
                 lhs = (P2, P4, P6)[d - 1]
                 wait("pe", ready[lhs])
+                wait("pe", ("r1_%d" % ((j - d) % (WIN - 1)), ENG1))
                 mm = g.tensor.matmul(ps(0), blk(T.mats, lhs, F), blk(T.cq, d), d == 1, d == nsrc)
             mm.then_inc(T.sem[m], 1)
-            wait("ve", ("c_arr", 16 // LANES))
+            wait("ve", ("c_arr", per))
             wait("ve", (m, 1))
             g.vector.tensor_tensor(T.sq[:, :], ps(0), blk(T.cq, 0), AluOpType.add).then_inc(T.sem.sq_done, 1)
-            g.wait_ge(T.sem.sq_done, 1)
+            wait("g", ("sq_done", 1))
             src = T.sq[:, :]
         else:
             src = blk(T.cq, 0)
 
         to = [cores[j + 1 + WIN * m] for m in use]
         g.remote_dma_fused([RemoteDMATransfer(
-            dst_ids=[dst_of(c) for c in to], dma_engine_mask=engines(to, 0, 8),
+            dst_ids=[dst_of(c) for c in to], dma_engine_mask=engines(to, ENG2),
             remote_sem=T.sem["s%d_%d" % (j // WIN, q)],
             srcs=[src], dsts=[blk(T.sland, m * LANES + q) for m in use], alu_op=0)], local_sem=T.sem.sent)
-        sent += 8
+        sent += ENG2
         g.wait_ge(T.sem.sent, sent)
         return
 
     r = rank
-    need_at = r >= 1
-    g.sync.dma_start(blk(T.mats, P1, F), T.a[:, :]).then_inc(T.sem.ld_a, 16)
-    if need_at:
-        g.scalar.dma_start(blk(T.mats, Q1, F), T.at[:, :]).then_inc(T.sem.ld_a, 16)
-    g.sync.dma_start(T.xs[:, 0:B], T.x[:, 0:B]).then_inc(T.sem.ld_x0, 16)
-    g.scalar.dma_start(T.xs[:, B:2 * B], T.x[:, B:2 * B]).then_inc(T.sem.ld_x1, 16)
-    got_a = ("ld_a", 32 if need_at else 16)
-    ready[Q1] = ready[P1] = got_a
-
-    sent = 0
-    per = 16 // LANES
+    nm = len([m for m in range(3) if r - 1 - WIN * m >= 0])
     mine = lanes_of(r) if r <= n - 2 else []
-    if mine and r >= 1:
-        g.wait_ge(T.sem[got_a[0]], got_a[1])
-        g.remote_dma_fused([RemoteDMATransfer(
-            dst_ids=[dst_of(c)], dma_engine_mask=engines([c], per * q, per), remote_sem=T.sem.a_arr,
-            srcs=[blk(T.mats, Q1, F, 2)], dsts=[blk(T.mats, Q1, F, 2)], alu_op=0)
-            for q, c in enumerate(mine)], local_sem=T.sem.sent)
-        sent += 16
+    feed = bool(mine) and r >= 1
+    need_at = feed or nm >= 2
+    g.sync.dma_start(blk(T.mats, P1, F), T.a[:, :]).then_inc(T.sem.ld_a, 16)
+    g.scalar.dma_start(T.xs[:, B:2 * B], T.x[:, B:2 * B]).then_inc(T.sem.ld_x1, 16)
+    g.sync.dma_start(T.xs[:, 0:B], T.x[:, 0:B]).then_inc(T.sem.ld_x0, 16)
+    if need_at:
+        g.scalar.dma_start(blk(T.mats, Q1, F), T.at[:, :]).then_inc(T.sem.ld_at, 16)
+    ready[P1] = ("ld_a", 16)
+    ready[Q1] = ("ld_at", 16)
 
-    wait("pe", got_a)
-    wait("pe", ("ld_x0", 16))
-    wait("ve", ("ld_x1", 16))
-    for q in range(LANES):
-        m = fresh()
-        g.tensor.matmul(ps(q), blk(T.mats, P1, F), blk(T.xs, q), True, True).then_inc(T.sem[m], 1)
-        wait("ve", (m, 1))
-        g.vector.tensor_tensor(blk(T.cs, q), ps(q), blk(T.xs, LANES + q), AluOpType.add).then_inc(T.sem.c_done, 1)
-        bank_free[q] = ("c_done", LANES)
+    def lane_engines(q):
+        c = mine[q]
+        same = topo.die(c) == topo.die(core)
+        k = [x for x in mine if (topo.die(x) == topo.die(core)) == same].index(c)
+        bits = bits_of([c])
+        return sum(bits[2 * per * k + (1 if same else 0) + 2 * i] for i in range(per))
+
+    sent = [0]
+
+    def to_lanes(src_of, dst_ap_of, sem):
+        g.remote_dma_fused([RemoteDMATransfer(
+            dst_ids=[dst_of(mine[q])], dma_engine_mask=lane_engines(q), remote_sem=sem,
+            srcs=[src_of(q)], dsts=[dst_ap_of(q)], alu_op=0) for q in range(LANES)], local_sem=T.sem.sent)
+        sent[0] += per * LANES
 
     if mine:
-        g.wait_ge(T.sem.c_done, LANES)
-        g.remote_dma_fused([RemoteDMATransfer(
-            dst_ids=[dst_of(c)], dma_engine_mask=engines([c], per * q, per), remote_sem=T.sem.c_arr,
-            srcs=[blk(T.cs, q)], dsts=[blk(T.cq, 0)], alu_op=0)
-            for q, c in enumerate(mine)], local_sem=T.sem.sent)
-        sent += 16
+        wait("g", ready[P1])
+        to_lanes(lambda q: a_part(r, q), lambda q: a_part(r, q), T.sem.a0)
+
+    wait("pe", ready[P1])
+    wait("pe", ("ld_x0", 16))
+    wait("ve", ("ld_x1", 16))
+    c_all = ("c_done", LANES)
+    if mine:
+        for q in range(LANES):
+            m = fresh()
+            g.tensor.matmul(ps(q), blk(T.mats, P1, F), blk(T.xs, q), True, True).then_inc(T.sem[m], 1)
+            wait("ve", (m, 1))
+            g.vector.tensor_tensor(blk(T.cs, q), ps(q), blk(T.xs, LANES + q), AluOpType.add).then_inc(T.sem.c_done, 1)
+            bank_free[q] = c_all
+        wait("g", c_all)
+        to_lanes(lambda q: blk(T.cs, q), lambda q: blk(T.cq, 0), T.sem.c_arr)
+    if feed:
+        wait("g", ready[Q1])
+        to_lanes(lambda q: blk(T.mats, Q1, F), lambda q: blk(T.mats, Q1, F), T.sem.a1)
 
     if r == 0:
-        g.sync.wait_ge(T.sem.ld_x0, 16)
+        wait("sy", ("ld_x0", 16))
         g.sync.dma_start(T.y[:, 0:B], T.xs[:, 0:B]).then_inc(T.sem.st, 16)
-        g.scalar.wait_ge(T.sem.c_done, LANES)
+        wait("sc", c_all)
         g.scalar.dma_start(T.y[:, B:2 * B], T.cs[:, :]).then_inc(T.sem.st, 16)
-        g.wait_ge(T.sem.sent, sent)
+        g.wait_ge(T.sem.sent, sent[0])
         g.wait_ge(T.sem.st, 32)
         return
 
-    nm = len([m for m in range(3) if r - 1 - WIN * m >= 0])
-    power(4, Q1, P1, 1, P2)
     if nm >= 2:
-        power(5, P1, Q1, 1, Q2)
-        power(6, Q2, P2, 1, P4)
-        power(7, P2, Q2, 1, Q4)
-        power(4, P4, Q4, 1, Q8)
-        power(5, Q8, P1, 2, P9)
+        power(4, Q1, P1, P2)
+        power(5, P1, Q1, Q2)
+        power(6, Q2, P2, P4)
+        power(7, P2, Q2, Q4)
+        power(4, P4, Q4, Q8)
+        power(5, Q8, P1, P9)
     if nm >= 3:
-        power(6, Q8, P9, 2, P17)
+        power(6, Q8, P9, P17)
 
-    fin = {}
-    for m in reversed(range(nm)):
+    pe0, ve0, pe1, ve1 = ([(fresh(), 1) for q in range(LANES)] for k in range(4))
+    for m in range(nm):
         jsrc = r - 1 - WIN * m
-        for inst in range(2):
-            for q in range(LANES):
-                bank = inst * LANES + q
-                lhs = P1 + 2 * m + inst
-                wait("pe", ready[lhs])
-                if bank in bank_free:
-                    wait("pe", bank_free[bank])
-                wait("pe", ("s%d_%d" % (jsrc // WIN, q), 8))
-                mm = g.tensor.matmul(ps(bank), blk(T.mats, lhs, F), blk(T.sland, m * LANES + q), m == nm - 1, m == 0)
-                if m == 0:
-                    fin[bank] = fresh()
-                    mm.then_inc(T.sem[fin[bank]], 1)
-    wait("ve", ("ld_x0", 16))
-    wait("ve", ("c_done", LANES))
-    for inst in range(2):
+        lhs = (P1, P9, P17)[m]
+        wait("pe", ready[lhs])
         for q in range(LANES):
-            bank = inst * LANES + q
-            wait("ve", (fin[bank], 1))
-            local = blk(T.xs, q) if inst == 0 else blk(T.cs, q)
-            g.vector.tensor_tensor(blk(T.ys, bank), ps(bank), local, AluOpType.add).then_inc(
-                T.sem.y0_done if inst == 0 else T.sem.y1_done, 1)
-    g.sync.wait_ge(T.sem.y0_done, LANES)
-    g.sync.dma_start(T.y[:, 0:B], T.ys[:, 0:B]).then_inc(T.sem.st, 16)
-    g.scalar.wait_ge(T.sem.y1_done, LANES)
-    g.scalar.dma_start(T.y[:, B:2 * B], T.ys[:, B:2 * B]).then_inc(T.sem.st, 16)
-    if sent:
-        g.wait_ge(T.sem.sent, sent)
-    g.wait_ge(T.sem.st, 32)
+            if q in bank_free:
+                wait("pe", bank_free[q])
+            wait("pe", ("s%d_%d" % (jsrc // WIN, q), ENG2))
+            mm = g.tensor.matmul(ps(q), blk(T.mats, lhs, F), blk(T.sland, m * LANES + q), m == 0, m == nm - 1)
+            if m == nm - 1:
+                mm.then_inc(T.sem[pe0[q][0]], 1)
+    wait("ve", ("ld_x0", 16))
+    for q in range(LANES):
+        wait("ve", pe0[q])
+        g.vector.tensor_tensor(blk(T.ys, q), ps(q), blk(T.xs, q), AluOpType.add).then_inc(T.sem[ve0[q][0]], 1)
+    for q in range(LANES):
+        bank = LANES + q
+        if bank in bank_free:
+            wait("pe", bank_free[bank])
+        wait("pe", ve0[q])
+        g.tensor.matmul(ps(bank), blk(T.mats, P1, F), blk(T.ys, q), True, True).then_inc(T.sem[pe1[q][0]], 1)
+        wait("ve", pe1[q])
+        g.vector.tensor_tensor(blk(T.ys, bank), ps(bank), blk(T.xs, bank), AluOpType.add).then_inc(T.sem[ve1[q][0]], 1)
+    half = LANES // 2
+    for k, done in enumerate((ve0[:half], ve0[half:], ve1[:half], ve1[half:])):
+        qn = ("sy", "sc")[k % 2]
+        for dep in done:
+            wait(qn, dep)
+        queues[qn].dma_start(blk(T.y, k, half * W), blk(T.ys, k, half * W)).then_inc(T.sem.st, 16)
+    if sent[0]:
+        g.wait_ge(T.sem.sent, sent[0])
+    g.wait_ge(T.sem.st, 64)

@@ -1,32 +1,33 @@
 from concourse.bass import DstId, RemoteDMATransfer
-from concourse.mybir import AluOpType
+from concourse.mybir import AluOpType, ActivationFunctionType
 
 LANES = 4
 WIN = 4
 B = 512
 W = B // LANES
 F = 128
-NPOOL = 48
+NPOOL = 64
 ENGS = 8
 ENG1 = 8
 ENG2 = 8
 
-Q1, P1, P2, P9, P17, Q2, P4, Q4, Q8 = range(9)
+Q1, P1, P2, P9, P17, Q2, P4, Q4, Q8, EYE = range(10)
 P6 = Q4
 
 SCRATCH = {
-    "mats": ("sbuf", [F, 9 * F], "bfloat16"),
+    "mats": ("sbuf", [F, 10 * F], "bfloat16"),
     "xs": ("sbuf", [F, 2 * B], "bfloat16"),
     "cs": ("sbuf", [F, B], "bfloat16"),
     "sland": ("sbuf", [F, 3 * B], "bfloat16"),
     "ys": ("sbuf", [F, 2 * B], "bfloat16"),
     "cq": ("sbuf", [F, WIN * W], "bfloat16"),
     "sq": ("sbuf", [F, W], "bfloat16"),
+    "msq": ("sbuf", [F, W], "bfloat16"),
 }
 for _b in range(8):
     SCRATCH["ps%d" % _b] = ("psum", [F, 512], "float32")
 
-SEMAPHORES = (["ld_a", "ld_at", "ld_x0", "ld_x1", "c_done", "st", "sent", "a0", "a1", "c_arr", "sq_done"]
+SEMAPHORES = (["ld_a", "ld_at", "ld_x0", "ld_x1", "c_done", "st", "sent", "a0", "a1", "i1", "c_arr", "sq_done", "ms_done"]
               + ["r1_%d" % k for k in range(WIN - 1)]
               + ["s%d_%d" % (k, q) for k in range(3) for q in range(LANES)]
               + ["k%d" % i for i in range(NPOOL)])
@@ -46,15 +47,13 @@ def rank_program(g, core, T, topo):
         cand.sort(key=lambda c: (topo.die(c) != topo.die(home), c))
         return cand[:LANES]
 
-    def a_part(j, q):
+    def eye_part(j, q):
         pos = q % 2
         if j == 0:
-            lo, wd = F // 2, F // 2
-        elif j == 1:
-            lo, wd = pos * (F // 4), F // 4
-        else:
-            lo, wd = pos * (F // 2), F // 2
-        return T.mats[:, P1 * F + lo:P1 * F + lo + wd]
+            return F // 2, F // 2
+        if j == 1:
+            return pos * (F // 4), F // 4
+        return pos * (F // 2), F // 2
 
     def bits_of(dsts):
         m = topo.mask(core, dsts[0])
@@ -114,12 +113,27 @@ def rank_program(g, core, T, topo):
         use = [m for m in reversed(range(3)) if j + 1 + WIN * m <= n - 1]
         sent = 0
 
-        onto = lanes_of(1)[q] if j == 0 else lanes_of(j)[q + 1 - 2 * (q % 2)]
-        wait("g", ("a0", per))
+        lo, wd = eye_part(j, q)
+        part = T.mats[:, EYE * F + lo:EYE * F + lo + wd]
+        ones, built = (fresh(), 1), (fresh(), 1)
+        g.vector.memset(part, 1.0).then_inc(T.sem[ones[0]], 1)
+        wait("g", ones)
+        g.affine_select(part, part, [[-1, wd]], AluOpType.is_equal, 0.0, -lo, 1).then_inc(T.sem[built[0]], 1)
+        wait("g", built)
+        mate = q + 1 - 2 * (q % 2)
+        onto = lanes_of(1)[q] if j == 0 else lanes_of(j)[mate]
         g.remote_dma_fused([RemoteDMATransfer(
-            dst_ids=[dst_of(onto)], dma_engine_mask=engines([onto, cores[j + 1]], ENGS), remote_sem=T.sem.a1,
-            srcs=[a_part(j, q)], dsts=[a_part(j, q)], alu_op=0)], local_sem=T.sem.sent)
+            dst_ids=[dst_of(onto)], dma_engine_mask=engines([onto, cores[j + 1]], ENGS), remote_sem=T.sem.i1,
+            srcs=[part], dsts=[part], alu_op=0)], local_sem=T.sem.sent)
         sent += ENGS
+
+        if q % 2 == 0 and j != 1:
+            onto = lanes_of(1)[mate] if j == 0 else lanes_of(j)[mate]
+            wait("g", ("a0", 2 * per))
+            g.remote_dma_fused([RemoteDMATransfer(
+                dst_ids=[dst_of(onto)], dma_engine_mask=engines([onto, cores[j + 1]], ENGS), remote_sem=T.sem.a1,
+                srcs=[blk(T.mats, P1, F)], dsts=[blk(T.mats, P1, F)], alu_op=0)], local_sem=T.sem.sent)
+            sent += ENGS
 
         wait("g", ("c_arr", per))
         if nxt:
@@ -131,46 +145,59 @@ def rank_program(g, core, T, topo):
             sent += ENG1
 
         if nsrc:
-            wait("pe", ("a0", per))
-            ready[Q1] = ready[P1] = ("a1", ENGS * (2 if j == 1 else 1) + per)
-            power(4, Q1, P1, P2)
+            ready[P1] = ("a0", 2 * per) if q % 2 == 0 else ("a1", ENGS)
+            wait("pe", built)
+            ready[EYE] = ("i1", ENGS * (2 if j == 1 else 1))
+            power(4, P1, EYE, Q1)
+            power(5, Q1, P1, P2)
             if nsrc >= 2:
-                power(5, P1, Q1, Q2)
-                power(6, Q2, P2, P4)
+                power(6, P1, Q1, Q2)
+                power(7, Q2, P2, P4)
             if nsrc >= 3:
-                power(7, Q2, P4, P6)
-            m = fresh()
+                power(4, Q2, P4, P6)
+            done = fresh()
             for d in range(1, nsrc + 1):
                 lhs = (P2, P4, P6)[d - 1]
                 wait("pe", ready[lhs])
                 wait("pe", ("r1_%d" % ((j - d) % (WIN - 1)), ENG1))
                 mm = g.tensor.matmul(ps(0), blk(T.mats, lhs, F), blk(T.cq, d), d == 1, d == nsrc)
-            mm.then_inc(T.sem[m], 1)
+            mm.then_inc(T.sem[done], 1)
             wait("ve", ("c_arr", per))
-            wait("ve", (m, 1))
+            wait("ve", (done, 1))
             g.vector.tensor_tensor(T.sq[:, :], ps(0), blk(T.cq, 0), AluOpType.add).then_inc(T.sem.sq_done, 1)
-            wait("g", ("sq_done", 1))
-            src = T.sq[:, :]
-        else:
-            src = blk(T.cq, 0)
 
-        to = [cores[j + 1 + WIN * m] for m in use]
-        g.remote_dma_fused([RemoteDMATransfer(
-            dst_ids=[dst_of(c) for c in to], dma_engine_mask=engines(to, ENG2),
-            remote_sem=T.sem["s%d_%d" % (j // WIN, q)],
-            srcs=[src], dsts=[blk(T.sland, m * LANES + q) for m in use], alu_op=0)], local_sem=T.sem.sent)
-        sent += ENG2
+        def hop2(src, ms):
+            to = [cores[j + 1 + WIN * m] for m in ms]
+            g.remote_dma_fused([RemoteDMATransfer(
+                dst_ids=[dst_of(c) for c in to], dma_engine_mask=engines(to, ENG2),
+                remote_sem=T.sem["s%d_%d" % (j // WIN, q)],
+                srcs=[src], dsts=[blk(T.sland, m * LANES + q) for m in ms], alu_op=0)], local_sem=T.sem.sent)
+            return ENG2
+
+        if nsrc:
+            far = [m for m in use if m >= 1]
+            if far:
+                wait("g", ("sq_done", 1))
+                sent += hop2(T.sq[:, :], far)
+            done = fresh()
+            wait("pe", ("sq_done", 1))
+            g.tensor.matmul(ps(1), blk(T.mats, P1, F), T.sq[:, :], True, True).then_inc(T.sem[done], 1)
+            wait("ve", (done, 1))
+            g.vector.tensor_copy(T.msq[:, :], ps(1)).then_inc(T.sem.ms_done, 1)
+            wait("g", ("ms_done", 1))
+            sent += hop2(T.msq[:, :], [0])
+        else:
+            sent += hop2(blk(T.cq, 0), use)
         g.wait_ge(T.sem.sent, sent)
         return
 
     r = rank
     nm = len([m for m in range(3) if r - 1 - WIN * m >= 0])
     mine = lanes_of(r) if r <= n - 2 else []
-    feed = bool(mine) and r >= 1
-    need_at = feed or nm >= 2
+    need_at = nm >= 2
     g.sync.dma_start(blk(T.mats, P1, F), T.a[:, :]).then_inc(T.sem.ld_a, 16)
-    g.scalar.dma_start(T.xs[:, B:2 * B], T.x[:, B:2 * B]).then_inc(T.sem.ld_x1, 16)
-    g.sync.dma_start(T.xs[:, 0:B], T.x[:, 0:B]).then_inc(T.sem.ld_x0, 16)
+    g.scalar.dma_start(T.xs[:, 0:B], T.x[:, 0:B]).then_inc(T.sem.ld_x0, 16)
+    g.sync.dma_start(T.xs[:, B:2 * B], T.x[:, B:2 * B]).then_inc(T.sem.ld_x1, 16)
     if need_at:
         g.scalar.dma_start(blk(T.mats, Q1, F), T.at[:, :]).then_inc(T.sem.ld_at, 16)
     ready[P1] = ("ld_a", 16)
@@ -185,15 +212,15 @@ def rank_program(g, core, T, topo):
 
     sent = [0]
 
-    def to_lanes(src_of, dst_ap_of, sem):
+    def to_lanes(step, src_of, dst_ap_of, sem):
         g.remote_dma_fused([RemoteDMATransfer(
-            dst_ids=[dst_of(mine[q])], dma_engine_mask=lane_engines(q), remote_sem=sem,
-            srcs=[src_of(q)], dsts=[dst_ap_of(q)], alu_op=0) for q in range(LANES)], local_sem=T.sem.sent)
+            dst_ids=[dst_of(mine[q])], dma_engine_mask=sum(lane_engines(q + i) for i in range(step)), remote_sem=sem,
+            srcs=[src_of(q)], dsts=[dst_ap_of(q)], alu_op=0) for q in range(0, LANES, step)], local_sem=T.sem.sent)
         sent[0] += per * LANES
 
     if mine:
         wait("g", ready[P1])
-        to_lanes(lambda q: a_part(r, q), lambda q: a_part(r, q), T.sem.a0)
+        to_lanes(2, lambda q: blk(T.mats, P1, F), lambda q: blk(T.mats, P1, F), T.sem.a0)
 
     wait("pe", ready[P1])
     wait("pe", ("ld_x0", 16))
@@ -207,12 +234,11 @@ def rank_program(g, core, T, topo):
             g.vector.tensor_tensor(blk(T.cs, q), ps(q), blk(T.xs, LANES + q), AluOpType.add).then_inc(T.sem.c_done, 1)
             bank_free[q] = c_all
         wait("g", c_all)
-        to_lanes(lambda q: blk(T.cs, q), lambda q: blk(T.cq, 0), T.sem.c_arr)
-    if feed:
-        wait("g", ready[Q1])
-        to_lanes(lambda q: blk(T.mats, Q1, F), lambda q: blk(T.mats, Q1, F), T.sem.a1)
+        to_lanes(1, lambda q: blk(T.cs, q), lambda q: blk(T.cq, 0), T.sem.c_arr)
 
     if r == 0:
+        wait("sy", ("sent", sent[0]))
+        wait("sc", ("sent", sent[0]))
         wait("sy", ("ld_x0", 16))
         g.sync.dma_start(T.y[:, 0:B], T.xs[:, 0:B]).then_inc(T.sem.st, 16)
         wait("sc", c_all)
@@ -220,6 +246,13 @@ def rank_program(g, core, T, topo):
         g.wait_ge(T.sem.sent, sent[0])
         g.wait_ge(T.sem.st, 32)
         return
+
+    ones, eye = (fresh(), 1), (fresh(), 1)
+    g.vector.memset(blk(T.mats, EYE, F), 1.0).then_inc(T.sem[ones[0]], 1)
+    wait("g", ones)
+    g.affine_select(blk(T.mats, EYE, F), blk(T.mats, EYE, F), [[-1, F]], AluOpType.is_equal, 0.0, 0, 1
+                    ).then_inc(T.sem[eye[0]], 1)
+    ready[EYE] = eye
 
     if nm >= 2:
         power(4, Q1, P1, P2)
@@ -231,33 +264,41 @@ def rank_program(g, core, T, topo):
     if nm >= 3:
         power(6, Q8, P9, P17)
 
-    pe0, ve0, pe1, ve1 = ([(fresh(), 1) for q in range(LANES)] for k in range(4))
-    for m in range(nm):
+    raw = [m for m in reversed(range(nm)) if m >= 1 or r == 1]
+    pe0, ve0, pe1, ac1 = ([(fresh(), 1) for q in range(LANES)] for k in range(4))
+    wait("pe", ready[EYE])
+    wait("pe", ("ld_x1", 16))
+    for k in range(2 * LANES):
+        if k in bank_free:
+            wait("pe", bank_free[k])
+        mm = g.tensor.matmul(ps(k), blk(T.mats, EYE, F), blk(T.xs, k), True, k < LANES and not raw)
+        if k < LANES and not raw:
+            mm.then_inc(T.sem[pe0[k][0]], 1)
+    for m in raw:
         jsrc = r - 1 - WIN * m
         lhs = (P1, P9, P17)[m]
         wait("pe", ready[lhs])
         for q in range(LANES):
-            if q in bank_free:
-                wait("pe", bank_free[q])
             wait("pe", ("s%d_%d" % (jsrc // WIN, q), ENG2))
-            mm = g.tensor.matmul(ps(q), blk(T.mats, lhs, F), blk(T.sland, m * LANES + q), m == 0, m == nm - 1)
-            if m == nm - 1:
+            mm = g.tensor.matmul(ps(q), blk(T.mats, lhs, F), blk(T.sland, m * LANES + q), False, m == raw[-1])
+            if m == raw[-1]:
                 mm.then_inc(T.sem[pe0[q][0]], 1)
-    wait("ve", ("ld_x0", 16))
     for q in range(LANES):
         wait("ve", pe0[q])
-        g.vector.tensor_tensor(blk(T.ys, q), ps(q), blk(T.xs, q), AluOpType.add).then_inc(T.sem[ve0[q][0]], 1)
+        if r == 1:
+            op = g.vector.tensor_copy(blk(T.ys, q), ps(q))
+        else:
+            wait("ve", ("s%d_%d" % ((r - 1) // WIN, q), ENG2))
+            op = g.vector.tensor_tensor(blk(T.ys, q), ps(q), blk(T.sland, q), AluOpType.add)
+        op.then_inc(T.sem[ve0[q][0]], 1)
     for q in range(LANES):
         bank = LANES + q
-        if bank in bank_free:
-            wait("pe", bank_free[bank])
         wait("pe", ve0[q])
-        g.tensor.matmul(ps(bank), blk(T.mats, P1, F), blk(T.ys, q), True, True).then_inc(T.sem[pe1[q][0]], 1)
-        wait("ve", pe1[q])
-        g.vector.tensor_tensor(blk(T.ys, bank), ps(bank), blk(T.xs, bank), AluOpType.add).then_inc(T.sem[ve1[q][0]], 1)
+        g.tensor.matmul(ps(bank), blk(T.mats, P1, F), blk(T.ys, q), False, True).then_inc(T.sem[pe1[q][0]], 1)
+        wait("sc", pe1[q])
+        g.scalar.activation(blk(T.ys, bank), ps(bank), ActivationFunctionType.Copy).then_inc(T.sem[ac1[q][0]], 1)
     half = LANES // 2
-    for k, done in enumerate((ve0[:half], ve0[half:], ve1[:half], ve1[half:])):
-        qn = ("sy", "sc")[k % 2]
+    for k, (qn, done) in enumerate((("sy", ve0[:half]), ("sy", ve0[half:]), ("sy", ac1[:half]), ("sc", ac1[half:]))):
         for dep in done:
             wait(qn, dep)
         queues[qn].dma_start(blk(T.y, k, half * W), blk(T.ys, k, half * W)).then_inc(T.sem.st, 16)

from concourse.bass import DstId, RemoteDMATransfer
from concourse.mybir import AluOpType, ActivationFunctionType

LANES = 4
WIN = 4
B = 512
W = B // LANES
F = 128
NPOOL = 64
ENGS = 8
ENG1 = 8
ENG2 = 8

Q1, P1, P2, P9, P17, Q2, P4, Q4, Q8, EYE = range(10)
P6 = Q4

SCRATCH = {
    "mats": ("sbuf", [F, 10 * F], "bfloat16"),
    "xs": ("sbuf", [F, 2 * B], "bfloat16"),
    "cs": ("sbuf", [F, B], "bfloat16"),
    "sland": ("sbuf", [F, 3 * B], "bfloat16"),
    "ys": ("sbuf", [F, 2 * B], "bfloat16"),
    "cq": ("sbuf", [F, WIN * W], "bfloat16"),
    "sq": ("sbuf", [F, W], "bfloat16"),
    "msq": ("sbuf", [F, W], "bfloat16"),
}
for _b in range(8):
    SCRATCH["ps%d" % _b] = ("psum", [F, 512], "float32")

SEMAPHORES = (["ld_a", "ld_at", "ld_x0", "ld_x1", "c_done", "st", "sent", "a0", "a1", "i1", "c_arr", "sq_done", "ms_done"]
              + ["r1_%d" % k for k in range(WIN - 1)]
              + ["s%d_%d" % (k, q) for k in range(3) for q in range(LANES)]
              + ["k%d" % i for i in range(NPOOL)])


def rank_program(g, core, T, topo):
    cores = list(T.cores)
    n = len(cores)
    every = range(topo.CORES_PER_CHIP * topo.CHIPS)
    per = 16 // LANES

    def lanes_of(j):
        home = cores[j]
        cand = [c for c in every
                if topo.chip(c) == topo.chip(home) and c != home
                and all(topo.may_write(c, d) for d in cores if d != c)]
        cand.sort(key=lambda c: (topo.die(c) != topo.die(home), c))
        return cand[:LANES]

    def eye_part(j, q):
        pos = q % 2
        if j == 0:
            return F // 2, F // 2
        if j == 1:
            return pos * (F // 4), F // 4
        return pos * (F // 2), F // 2

    def bits_of(dsts):
        m = topo.mask(core, dsts[0])
        for d in dsts[1:]:
            m &= topo.mask(core, d)
        return [1 << i for i in range(m.bit_length()) if (m >> i) & 1]

    def engines(dsts, count):
        return sum(bits_of(dsts)[:count])

    def dst_of(c):
        rid, pid, _se = topo.addr(c)
        return DstId(rid=rid, pnc=pid)

    def blk(t, k, w=W, cnt=1):
        return t[:, k * w:(k + cnt) * w]

    pool = [0]
    queues = {"pe": g.tensor, "ve": g.vector, "g": g, "sy": g.sync, "sc": g.scalar}
    seen = set()
    ready = {}
    bank_free = {}

    def fresh():
        pool[0] += 1
        return "k%d" % (pool[0] - 1)

    def wait(q, dep):
        if (q, dep) not in seen:
            seen.add((q, dep))
            queues[q].wait_ge(T.sem[dep[0]], dep[1])

    def ps(b, cols=W):
        return T["ps%d" % b][:, 0:cols]

    def power(bank, lhs, rhs, out):
        wait("pe", ready[lhs])
        wait("pe", ready[rhs])
        if bank in bank_free:
            wait("pe", bank_free[bank])
        m, d = fresh(), fresh()
        g.tensor.matmul(ps(bank, F), blk(T.mats, lhs, F), blk(T.mats, rhs, F), True, True).then_inc(T.sem[m], 1)
        wait("ve", (m, 1))
        g.vector.tensor_copy(blk(T.mats, out, F), ps(bank, F)).then_inc(T.sem[d], 1)
        ready[out] = (d, 1)
        bank_free[bank] = (d, 1)

    rank = T.rank_of(core)

    if rank is None:
        where = [(j, q) for j in range(n - 1) for q, c in enumerate(lanes_of(j)) if c == core]
        if not where:
            return
        j, q = where[0]
        nsrc = min(WIN - 1, j)
        nxt = [d for d in range(1, WIN) if j + d <= n - 2]
        use = [m for m in reversed(range(3)) if j + 1 + WIN * m <= n - 1]
        sent = 0

        lo, wd = eye_part(j, q)
        part = T.mats[:, EYE * F + lo:EYE * F + lo + wd]
        ones, built = (fresh(), 1), (fresh(), 1)
        g.vector.memset(part, 1.0).then_inc(T.sem[ones[0]], 1)
        wait("g", ones)
        g.affine_select(part, part, [[-1, wd]], AluOpType.is_equal, 0.0, -lo, 1).then_inc(T.sem[built[0]], 1)
        wait("g", built)
        mate = q + 1 - 2 * (q % 2)
        onto = lanes_of(1)[q] if j == 0 else lanes_of(j)[mate]
        g.remote_dma_fused([RemoteDMATransfer(
            dst_ids=[dst_of(onto)], dma_engine_mask=engines([onto, cores[j + 1]], ENGS), remote_sem=T.sem.i1,
            srcs=[part], dsts=[part], alu_op=0)], local_sem=T.sem.sent)
        sent += ENGS

        if q % 2 == 0 and j != 1:
            onto = lanes_of(1)[mate] if j == 0 else lanes_of(j)[mate]
            wait("g", ("a0", 2 * per))
            g.remote_dma_fused([RemoteDMATransfer(
                dst_ids=[dst_of(onto)], dma_engine_mask=engines([onto, cores[j + 1]], ENGS), remote_sem=T.sem.a1,
                srcs=[blk(T.mats, P1, F)], dsts=[blk(T.mats, P1, F)], alu_op=0)], local_sem=T.sem.sent)
            sent += ENGS

        wait("g", ("c_arr", per))
        if nxt:
            to = [lanes_of(j + d)[q] for d in nxt]
            g.remote_dma_fused([RemoteDMATransfer(
                dst_ids=[dst_of(c) for c in to], dma_engine_mask=engines(to, ENG1),
                remote_sem=T.sem["r1_%d" % (j % (WIN - 1))],
                srcs=[blk(T.cq, 0)], dsts=[blk(T.cq, d) for d in nxt], alu_op=0)], local_sem=T.sem.sent)
            sent += ENG1

        if nsrc:
            ready[P1] = ("a0", 2 * per) if q % 2 == 0 else ("a1", ENGS)
            wait("pe", built)
            ready[EYE] = ("i1", ENGS * (2 if j == 1 else 1))
            power(4, P1, EYE, Q1)
            power(5, Q1, P1, P2)
            if nsrc >= 2:
                power(6, P1, Q1, Q2)
                power(7, Q2, P2, P4)
            if nsrc >= 3:
                power(4, Q2, P4, P6)
            done = fresh()
            for d in range(1, nsrc + 1):
                lhs = (P2, P4, P6)[d - 1]
                wait("pe", ready[lhs])
                wait("pe", ("r1_%d" % ((j - d) % (WIN - 1)), ENG1))
                mm = g.tensor.matmul(ps(0), blk(T.mats, lhs, F), blk(T.cq, d), d == 1, d == nsrc)
            mm.then_inc(T.sem[done], 1)
            wait("ve", ("c_arr", per))
            wait("ve", (done, 1))
            g.vector.tensor_tensor(T.sq[:, :], ps(0), blk(T.cq, 0), AluOpType.add).then_inc(T.sem.sq_done, 1)

        def hop2(src, ms):
            to = [cores[j + 1 + WIN * m] for m in ms]
            g.remote_dma_fused([RemoteDMATransfer(
                dst_ids=[dst_of(c) for c in to], dma_engine_mask=engines(to, ENG2),
                remote_sem=T.sem["s%d_%d" % (j // WIN, q)],
                srcs=[src], dsts=[blk(T.sland, m * LANES + q) for m in ms], alu_op=0)], local_sem=T.sem.sent)
            return ENG2

        if nsrc:
            far = [m for m in use if m >= 1]
            if far:
                wait("g", ("sq_done", 1))
                sent += hop2(T.sq[:, :], far)
            done = fresh()
            wait("pe", ("sq_done", 1))
            g.tensor.matmul(ps(1), blk(T.mats, P1, F), T.sq[:, :], True, True).then_inc(T.sem[done], 1)
            wait("ve", (done, 1))
            g.vector.tensor_copy(T.msq[:, :], ps(1)).then_inc(T.sem.ms_done, 1)
            wait("g", ("ms_done", 1))
            sent += hop2(T.msq[:, :], [0])
        else:
            sent += hop2(blk(T.cq, 0), use)
        g.wait_ge(T.sem.sent, sent)
        return

    r = rank
    nm = len([m for m in range(3) if r - 1 - WIN * m >= 0])
    mine = lanes_of(r) if r <= n - 2 else []
    need_at = nm >= 2
    g.sync.dma_start(blk(T.mats, P1, F), T.a[:, :]).then_inc(T.sem.ld_a, 16)
    g.scalar.dma_start(T.xs[:, 0:B], T.x[:, 0:B]).then_inc(T.sem.ld_x0, 16)
    g.sync.dma_start(T.xs[:, B:2 * B], T.x[:, B:2 * B]).then_inc(T.sem.ld_x1, 16)
    if need_at:
        g.scalar.dma_start(blk(T.mats, Q1, F), T.at[:, :]).then_inc(T.sem.ld_at, 16)
    ready[P1] = ("ld_a", 16)
    ready[Q1] = ("ld_at", 16)

    def lane_engines(q):
        c = mine[q]
        same = topo.die(c) == topo.die(core)
        k = [x for x in mine if (topo.die(x) == topo.die(core)) == same].index(c)
        bits = bits_of([c])
        return sum(bits[2 * per * k + (1 if same else 0) + 2 * i] for i in range(per))

    sent = [0]

    def to_lanes(step, src_of, dst_ap_of, sem):
        g.remote_dma_fused([RemoteDMATransfer(
            dst_ids=[dst_of(mine[q])], dma_engine_mask=sum(lane_engines(q + i) for i in range(step)), remote_sem=sem,
            srcs=[src_of(q)], dsts=[dst_ap_of(q)], alu_op=0) for q in range(0, LANES, step)], local_sem=T.sem.sent)
        sent[0] += per * LANES

    if mine:
        wait("g", ready[P1])
        to_lanes(2, lambda q: blk(T.mats, P1, F), lambda q: blk(T.mats, P1, F), T.sem.a0)

    wait("pe", ready[P1])
    wait("pe", ("ld_x0", 16))
    wait("ve", ("ld_x1", 16))
    c_all = ("c_done", LANES)
    if mine:
        for q in range(LANES):
            m = fresh()
            g.tensor.matmul(ps(q), blk(T.mats, P1, F), blk(T.xs, q), True, True).then_inc(T.sem[m], 1)
            wait("ve", (m, 1))
            g.vector.tensor_tensor(blk(T.cs, q), ps(q), blk(T.xs, LANES + q), AluOpType.add).then_inc(T.sem.c_done, 1)
            bank_free[q] = c_all
        wait("g", c_all)
        to_lanes(1, lambda q: blk(T.cs, q), lambda q: blk(T.cq, 0), T.sem.c_arr)

    if r == 0:
        wait("sy", ("sent", sent[0]))
        wait("sc", ("sent", sent[0]))
        wait("sy", ("ld_x0", 16))
        g.sync.dma_start(T.y[:, 0:B], T.xs[:, 0:B]).then_inc(T.sem.st, 16)
        wait("sc", c_all)
        g.scalar.dma_start(T.y[:, B:2 * B], T.cs[:, :]).then_inc(T.sem.st, 16)
        g.wait_ge(T.sem.sent, sent[0])
        g.wait_ge(T.sem.st, 32)
        return

    ones, eye = (fresh(), 1), (fresh(), 1)
    g.vector.memset(blk(T.mats, EYE, F), 1.0).then_inc(T.sem[ones[0]], 1)
    wait("g", ones)
    g.affine_select(blk(T.mats, EYE, F), blk(T.mats, EYE, F), [[-1, F]], AluOpType.is_equal, 0.0, 0, 1
                    ).then_inc(T.sem[eye[0]], 1)
    ready[EYE] = eye

    if nm >= 2:
        power(4, Q1, P1, P2)
        power(5, P1, Q1, Q2)
        power(6, Q2, P2, P4)
        power(7, P2, Q2, Q4)
        power(4, P4, Q4, Q8)
        power(5, Q8, P1, P9)
    if nm >= 3:
        power(6, Q8, P9, P17)

    raw = [m for m in reversed(range(nm)) if m >= 1 or r == 1]
    pe0, ve0, pe1, ac1 = ([(fresh(), 1) for q in range(LANES)] for k in range(4))
    wait("pe", ready[EYE])
    wait("pe", ("ld_x1", 16))
    for k in range(2 * LANES):
        if k in bank_free:
            wait("pe", bank_free[k])
        mm = g.tensor.matmul(ps(k), blk(T.mats, EYE, F), blk(T.xs, k), True, k < LANES and not raw)
        if k < LANES and not raw:
            mm.then_inc(T.sem[pe0[k][0]], 1)
    for m in raw:
        jsrc = r - 1 - WIN * m
        lhs = (P1, P9, P17)[m]
        wait("pe", ready[lhs])
        for q in range(LANES):
            wait("pe", ("s%d_%d" % (jsrc // WIN, q), ENG2))
            mm = g.tensor.matmul(ps(q), blk(T.mats, lhs, F), blk(T.sland, m * LANES + q), False, m == raw[-1])
            if m == raw[-1]:
                mm.then_inc(T.sem[pe0[q][0]], 1)
    for q in range(LANES):
        wait("ve", pe0[q])
        if r == 1:
            op = g.vector.tensor_copy(blk(T.ys, q), ps(q))
        else:
            wait("ve", ("s%d_%d" % ((r - 1) // WIN, q), ENG2))
            op = g.vector.tensor_tensor(blk(T.ys, q), ps(q), blk(T.sland, q), AluOpType.add)
        op.then_inc(T.sem[ve0[q][0]], 1)
    for q in range(LANES):
        bank = LANES + q
        wait("pe", ve0[q])
        g.tensor.matmul(ps(bank), blk(T.mats, P1, F), blk(T.ys, q), False, True).then_inc(T.sem[pe1[q][0]], 1)
        wait("sc", pe1[q])
        g.scalar.activation(blk(T.ys, bank), ps(bank), ActivationFunctionType.Copy).then_inc(T.sem[ac1[q][0]], 1)
    half = LANES // 2
    for k, (qn, done) in enumerate((("sy", ve0[:half]), ("sy", ve0[half:]), ("sy", ac1[:half]), ("sc", ac1[half:]))):
        for dep in done:
            wait(qn, dep)
        queues[qn].dma_start(blk(T.y, k, half * W), blk(T.ys, k, half * W)).then_inc(T.sem.st, 16)
    if sent[0]:
        g.wait_ge(T.sem.sent, sent[0])
    g.wait_ge(T.sem.st, 64)
